import numpy as np
import ml_dtypes


def mxq(x, axis, fmt="e4m3"):
    dtype, down = {"e4m3": (ml_dtypes.float8_e4m3fn, 7), "e5m2": (ml_dtypes.float8_e5m2, 14)}[fmt]
    v = np.moveaxis(np.asarray(x, np.float32).astype(ml_dtypes.bfloat16).astype(np.float64), axis, -1)
    blocks = v.reshape(v.shape[:-1] + (-1, 32))
    amax = np.abs(blocks).max(-1, keepdims=True)
    byte = np.maximum(np.where(amax > 0, np.frexp(amax)[1] - 1 + 127, 0) - down, 1)
    scale = np.exp2(byte - 127.0)
    codes = (blocks / scale).astype(np.float32).astype(dtype).astype(np.float64)
    return np.moveaxis((codes * scale).reshape(v.shape), -1, axis)


WIDE = False


def mx_kscale(k):
    if not WIDE:
        return np.ones(k)
    levels = np.array([30, -30])
    if k % 512:
        return np.exp2(np.random.permutation(np.resize(levels, k // 32))).repeat(32)
    a = np.empty((k // 512, 16))
    for p in range(k // 512):
        a[p, :8] = np.random.permutation(np.resize(levels, 8))
        for g in range(8):
            far = levels[np.abs(levels - a[p, g]) >= 10]
            a[p, g + 8] = far[np.random.randint(len(far))]
    return np.exp2(a.ravel()).repeat(32)


def f64(x):
    return np.asarray(x).astype(np.float64)


def striped(idx):
    return np.tile(np.asarray(idx).reshape(-1, 16).T, (8, 1)).astype(np.uint16)


def unstriped(offs):
    return offs[:16].T.reshape(-1).astype(np.int64)


K, J, N, T, V = 256, 1024, 256, 2048, 2048


def setup_inputs():
    n = np.random.standard_normal
    idx = np.random.permutation(T)[:J]
    idx2 = np.random.permutation(T)[:J]
    idx3 = np.random.permutation(V)[:J]
    fj = mx_kscale(J)
    return {
        "xf": (n((K, T))).astype(np.float32),
        "ra": (np.random.uniform(0.5, 1.5, (1, J)) * fj).astype(np.float32),
        "gt": (n((N, V)) * np.exp(0.5 * n((1, V)))).astype(np.float32),
        "rb": (np.random.uniform(0.5, 1.5, (1, J)) / fj).astype(np.float32),
        "pr": (n((N, J))).astype(np.float32),
        "pc1": (np.random.uniform(0.02, 0.08, (K, N))).astype(np.float32),
        "old": (0.5 * n((K, N))).astype(np.float32),
        "offs": striped(idx),
        "offs2": striped(idx2),
        "offs3": striped(idx3),
    }


def reference(xf, ra, gt, rb, pr, pc1, old, offs, offs2, offs3):
    idx = unstriped(offs)
    idx2 = unstriped(offs2)
    idx3 = unstriped(offs3)
    us = (f64(xf)[:, idx] - f64(xf)[:, idx2]) * f64(ra)
    uj = us.T
    gs = (f64(gt)[:, idx3] - f64(pr)) * f64(rb)
    gj = gs.T
    ujq = mxq(uj, 0, "e4m3")
    gjq = mxq(gj, 0, "e5m2")
    w = ujq.T @ gjq
    w2 = w * f64(pc1)
    y = f64(old) - w2 + 0.2 * np.mean(w2, axis=1, keepdims=True)
    return y

@@ -1,0 +1,182 @@
+from contextlib import ExitStack
+
+import concourse.mybir as mybir
+from concourse.masks import make_identity
+
+K, J, N, T, V = 256, 1024, 256, 2048, 2048
+FLOPS = 2 * K * J * N
+
+F32 = mybir.dt.float32
+BF16 = mybir.dt.bfloat16
+U32 = mybir.dt.uint32
+U16 = mybir.dt.uint16
+U8 = mybir.dt.uint8
+E4M3X4 = mybir.dt.float8_e4m3fn_x4
+E5M2X4 = mybir.dt.float8_e5m2_x4
+ALU = mybir.AluOpType
+COPY = mybir.ActivationFunctionType.Copy
+
+P = 128
+PACK = 4
+PASS = P * PACK
+LIST_COLS = PASS // 16
+
+
+def tile_list_moment_gaps_errors_preconditioned_kernel(tc, xf, ra, gt, rb, pr, pc1, old, offs, offs2, offs3, out):
+    nc = tc.nc
+    with ExitStack() as ctx:
+        keep = ctx.enter_context(tc.tile_pool(name="keep", bufs=1))
+        psum = ctx.enter_context(tc.psum_pool(name="psum", bufs=1))
+
+        def list_slice(tile, a):
+            return tile[:, a * LIST_COLS : (a + 1) * LIST_COLS]
+
+        first = keep.tile([P, J // 16], U16, name="first")
+        second = keep.tile([P, J // 16], U16, name="second")
+        third = keep.tile([P, J // 16], U16, name="third")
+        x_tab = [keep.tile([P, T], F32, name=f"x_tab{h}") for h in range(2)]
+        g_tab = [keep.tile([P, V], F32, name=f"g_tab{h}") for h in range(2)]
+        pred = [[keep.tile([P, PASS], F32, name=f"pred{h}{a}") for a in range(2)] for h in range(2)]
+        ra_sb = keep.tile([P, 2, PACK], F32, name="ra_sb")
+        rb_sb = keep.tile([P, 2, PACK], F32, name="rb_sb")
+        rb_neg = keep.tile([P, 2, PACK], F32, name="rb_neg")
+        pc1_sb = keep.tile([P, 2, N], F32, name="pc1_sb")
+        old_sb = keep.tile([P, 2, N], F32, name="old_sb")
+        ident = keep.tile([P, P], F32, name="ident")
+
+        nc.scalar.dma_start(out=rb_sb[:], in_=rb.rearrange("o (a p t) -> p (o a) t", p=P, t=PACK))
+        nc.scalar.dma_start(out=ra_sb[:], in_=ra.rearrange("o (a p t) -> p (o a) t", p=P, t=PACK))
+        nc.sync.dma_start(out=x_tab[0][:], in_=xf[0:P, :])
+        nc.sync.dma_start(second[:], offs2)
+        nc.sync.dma_start(first[:], offs)
+        nc.sync.dma_start(out=x_tab[1][:], in_=xf[P : 2 * P, :])
+        nc.sync.dma_start(third[:], offs3)
+        nc.sync.dma_start(out=g_tab[0][:], in_=gt[0:P, :])
+        for a in range(2):
+            nc.sync.dma_start(out=pred[0][a][:], in_=pr[0:P, a * PASS : (a + 1) * PASS])
+        nc.sync.dma_start(out=g_tab[1][:], in_=gt[P : 2 * P, :])
+        for a in range(2):
+            nc.sync.dma_start(out=pred[1][a][:], in_=pr[P : 2 * P, a * PASS : (a + 1) * PASS])
+        nc.sync.dma_start(out=pc1_sb[:], in_=pc1.rearrange("(h p) n -> p h n", p=P))
+        nc.sync.dma_start(out=old_sb[:], in_=old.rearrange("(h p) n -> p h n", p=P))
+        make_identity(nc, ident[:])
+        nc.scalar.activation(out=rb_neg[:], in_=rb_sb[:], func=COPY, scale=-1.0)
+
+        def gather_scalar(name, table, offsets, scale, tag=""):
+            picked = keep.tile([P, PASS], F32, name=name, tag=tag or name, align_bytes=64)
+            nc.scalar.activation(out=picked[:], in_=table[:].indirect(offsets), func=COPY, scale=scale)
+            return picked
+
+        def gather_vector(name, table, offsets):
+            picked = keep.tile([P, PASS], F32, name=name)
+            nc.vector.tensor_copy(out=picked[:], in_=table[:].indirect(offsets))
+            return picked
+
+        def gather_minus(name, table, offsets, other):
+            diff = keep.tile([P, PASS], F32, name=name)
+            nc.vector.tensor_tensor(out=diff[:], in0=table[:].indirect(offsets), in1=other[:], op=ALU.subtract)
+            return diff
+
+        def subtract_dealt(name, left, right):
+            diff = keep.tile([P, PACK, P], F32, name=name)
+            nc.vector.tensor_tensor(
+                out=diff[:].rearrange("p t q -> p q t"),
+                in0=left[:].rearrange("p (q t) -> p q t", t=PACK),
+                in1=right[:].rearrange("p (q t) -> p q t", t=PACK),
+                op=ALU.subtract,
+            )
+            return diff
+
+        def stepped(tile, t):
+            return tile[:, t:PASS:PACK]
+
+        def turn(tag, sources):
+            bank = psum.tile([P, PACK, P], F32, name=tag)
+            count = len(sources) * PACK
+            done = 0
+            for source in sources:
+                for t in range(PACK):
+                    nc.tensor.matmul(
+                        out=bank[:, t, :], lhsT=source(t), rhs=ident[:], is_transpose=True,
+                        start=(done == 0), stop=(done == count - 1),
+                    )
+                    done += 1
+            return bank
+
+        def weigh(dest, bank, weights):
+            nc.vector.tensor_tensor(
+                out=dest.rearrange("p (c t) -> p c t", t=PACK),
+                in0=bank[:].rearrange("p t c -> p c t"),
+                in1=weights.unsqueeze(1).to_broadcast([P, P, PACK]),
+                op=ALU.mult,
+            )
+
+        u_codes = [keep.tile([P, K], U32, name=f"u_codes{a}", align_bytes=64) for a in range(2)]
+        u_scales = [keep.tile([P, K], U8, name=f"u_scales{a}", align_bytes=64) for a in range(2)]
+        g_codes = [[keep.tile([P, P], U32, name=f"g_codes{h}{a}", align_bytes=64) for a in range(2)] for h in range(2)]
+        g_scales = [[keep.tile([P, P], U8, name=f"g_scales{h}{a}", align_bytes=64) for a in range(2)] for h in range(2)]
+
+        b00 = gather_scalar("b00", x_tab[0], list_slice(second, 0), 1.0)
+        a01 = gather_vector("a01", x_tab[0], list_slice(first, 1))
+        nb01 = gather_scalar("nb01", x_tab[0], list_slice(second, 1), -1.0)
+        d00 = gather_minus("d00", x_tab[0], list_slice(first, 0), b00)
+        u01 = turn("u01", [lambda t: stepped(a01, t), lambda t: stepped(nb01, t)])
+        u00 = turn("u00", [lambda t: stepped(d00, t)])
+
+        b10 = gather_scalar("b10", x_tab[1], list_slice(second, 0), 1.0, tag="held")
+        a11 = gather_vector("a11", x_tab[1], list_slice(first, 1))
+        b11 = gather_scalar("b11", x_tab[1], list_slice(second, 1), 1.0)
+        d10 = gather_minus("d10", x_tab[1], list_slice(first, 0), b10)
+        d11 = subtract_dealt("d11", a11, b11)
+        u10 = turn("u10", [lambda t: stepped(d10, t)])
+        u11 = turn("u11", [lambda t: d11[:, t, :]])
+
+        u_bf = keep.tile([P, 2, 2 * PASS], BF16, name="u_bf", tag="held", align_bytes=64)
+        weigh(u_bf[:, 1, 0:PASS], u01, ra_sb[:, 1, :])
+        weigh(u_bf[:, 0, 0:PASS], u00, ra_sb[:, 0, :])
+        weigh(u_bf[:, 0, PASS : 2 * PASS], u10, ra_sb[:, 0, :])
+        weigh(u_bf[:, 1, PASS : 2 * PASS], u11, ra_sb[:, 1, :])
+        for a in range(2):
+            nc.vector.quantize_mx(out=u_codes[a][:].bitcast(E4M3X4), scales=u_scales[a][:], in_=u_bf[:, a, :])
+
+        for h in range(2):
+            ng0 = gather_scalar(f"ng{h}0", g_tab[h], list_slice(third, 0), -1.0)
+            g1 = gather_scalar(f"g{h}1", g_tab[h], list_slice(third, 1), 1.0)
+            bank0 = turn(f"e{h}0", [lambda t: stepped(pred[h][0], t), lambda t: stepped(ng0, t)])
+            e1 = subtract_dealt(f"e{h}1d", pred[h][1], g1)
+            bank1 = turn(f"e{h}1", [lambda t: e1[:, t, :]])
+            g_bf = [keep.tile([P, PASS], BF16, name=f"g_bf{h}{a}", align_bytes=64) for a in range(2)]
+            for a in range(2):
+                weigh(g_bf[a][:], [bank0, bank1][a], rb_neg[:, a, :])
+            for a in range(2):
+                nc.vector.quantize_mx(out=g_codes[h][a][:].bitcast(E5M2X4), scales=g_scales[h][a][:], in_=g_bf[a][:])
+
+        moment = [psum.tile([P, N], F32, name=f"moment{h}", tag=["u00", "u01"][h]) for h in range(2)]
+        for nh in range(2):
+            for h in range(2):
+                for a in range(2):
+                    nc.tensor.matmul_mx(
+                        out=moment[h][:, nh * P : (nh + 1) * P],
+                        lhsT=u_codes[a][:, h * P : (h + 1) * P].bitcast(E4M3X4),
+                        lhsT_scale=u_scales[a][:, h * P : (h + 1) * P],
+                        rhs=g_codes[nh][a][:].bitcast(E5M2X4),
+                        rhs_scale=g_scales[nh][a][:],
+                        start=(a == 0),
+                        stop=(a == 1),
+                    )
+        w2_neg = [keep.tile([P, N], F32, name=f"w2_neg{h}") for h in range(2)]
+        sums = [keep.tile([P, 1], F32, name=f"sums{h}") for h in range(2)]
+        shift = [keep.tile([P, 1], F32, name=f"shift{h}") for h in range(2)]
+        res = [keep.tile([P, N], F32, name=f"res{h}") for h in range(2)]
+        for h in range(2):
+            nc.vector.scalar_tensor_tensor(
+                out=w2_neg[h][:], in0=moment[h][:], scalar=-1.0, in1=pc1_sb[:, h, :],
+                op0=ALU.mult, op1=ALU.mult, accum_out=sums[h][:],
+            )
+        for h in range(2):
+            nc.vector.tensor_scalar(out=shift[h][:], in0=sums[h][:], scalar1=-0.2 / N, scalar2=None, op0=ALU.mult)
+        for h in range(2):
+            nc.vector.scalar_tensor_tensor(
+                out=res[h][:], in0=w2_neg[h][:], scalar=shift[h][:], in1=old_sb[:, h, :], op0=ALU.add, op1=ALU.add
+            )
+            [nc.sync, nc.scalar][h].dma_start(out=out[h * P : (h + 1) * P, :], in_=res[h][:])

@@ -36,7 +36,7 @@ def tile_list_moment_gaps_errors_preconditioned_kernel(tc, xf, ra, gt, rb, pr, p
         third = keep.tile([P, J // 16], U16, name="third")
         x_tab = [keep.tile([P, T], F32, name=f"x_tab{h}") for h in range(2)]
         g_tab = [keep.tile([P, V], F32, name=f"g_tab{h}") for h in range(2)]
-        pred = [[keep.tile([P, PASS], F32, name=f"pred{h}{a}") for a in range(2)] for h in range(2)]
+        pred = [[keep.tile([P, PASS], F32, name=f"pred{h}{a}", align_bytes=64) for a in range(2)] for h in range(2)]
         ra_sb = keep.tile([P, 2, PACK], F32, name="ra_sb")
         rb_sb = keep.tile([P, 2, PACK], F32, name="rb_sb")
         rb_neg = keep.tile([P, 2, PACK], F32, name="rb_neg")
@@ -68,7 +68,7 @@ def tile_list_moment_gaps_errors_preconditioned_kernel(tc, xf, ra, gt, rb, pr, p
             return picked
 
         def gather_vector(name, table, offsets):
-            picked = keep.tile([P, PASS], F32, name=name)
+            picked = keep.tile([P, PASS], F32, name=name, align_bytes=64)
             nc.vector.tensor_copy(out=picked[:], in_=table[:].indirect(offsets))
             return picked
 
@@ -111,10 +111,8 @@ def tile_list_moment_gaps_errors_preconditioned_kernel(tc, xf, ra, gt, rb, pr, p
                 op=ALU.mult,
             )
 
-        u_codes = [keep.tile([P, K], U32, name=f"u_codes{a}", align_bytes=64) for a in range(2)]
-        u_scales = [keep.tile([P, K], U8, name=f"u_scales{a}", align_bytes=64) for a in range(2)]
-        g_codes = [[keep.tile([P, P], U32, name=f"g_codes{h}{a}", align_bytes=64) for a in range(2)] for h in range(2)]
-        g_scales = [[keep.tile([P, P], U8, name=f"g_scales{h}{a}", align_bytes=64) for a in range(2)] for h in range(2)]
+        u_scales = keep.tile([P, 2, K], U8, name="u_scales", align_bytes=64)
+        g_scales = [keep.tile([P, 2, P], U8, name=f"g_scales{h}", align_bytes=64) for h in range(2)]
 
         b00 = gather_scalar("b00", x_tab[0], list_slice(second, 0), 1.0)
         a01 = gather_vector("a01", x_tab[0], list_slice(first, 1))
@@ -123,7 +121,7 @@ def tile_list_moment_gaps_errors_preconditioned_kernel(tc, xf, ra, gt, rb, pr, p
         u01 = turn("u01", [lambda t: stepped(a01, t), lambda t: stepped(nb01, t)])
         u00 = turn("u00", [lambda t: stepped(d00, t)])
 
-        b10 = gather_scalar("b10", x_tab[1], list_slice(second, 0), 1.0, tag="held")
+        b10 = gather_scalar("b10", x_tab[1], list_slice(second, 0), 1.0)
         a11 = gather_vector("a11", x_tab[1], list_slice(first, 1))
         b11 = gather_scalar("b11", x_tab[1], list_slice(second, 1), 1.0)
         d10 = gather_minus("d10", x_tab[1], list_slice(first, 0), b10)
@@ -131,25 +129,47 @@ def tile_list_moment_gaps_errors_preconditioned_kernel(tc, xf, ra, gt, rb, pr, p
         u10 = turn("u10", [lambda t: stepped(d10, t)])
         u11 = turn("u11", [lambda t: d11[:, t, :]])
 
-        u_bf = keep.tile([P, 2, 2 * PASS], BF16, name="u_bf", tag="held", align_bytes=64)
+        u_bf = keep.tile([P, 2, 2 * PASS], BF16, name="u_bf", tag="a11", align_bytes=64)
         weigh(u_bf[:, 1, 0:PASS], u01, ra_sb[:, 1, :])
         weigh(u_bf[:, 0, 0:PASS], u00, ra_sb[:, 0, :])
         weigh(u_bf[:, 0, PASS : 2 * PASS], u10, ra_sb[:, 0, :])
         weigh(u_bf[:, 1, PASS : 2 * PASS], u11, ra_sb[:, 1, :])
-        for a in range(2):
-            nc.vector.quantize_mx(out=u_codes[a][:].bitcast(E4M3X4), scales=u_scales[a][:], in_=u_bf[:, a, :])
 
-        for h in range(2):
+        def error_banks(h):
             ng0 = gather_scalar(f"ng{h}0", g_tab[h], list_slice(third, 0), -1.0)
             g1 = gather_scalar(f"g{h}1", g_tab[h], list_slice(third, 1), 1.0)
             bank0 = turn(f"e{h}0", [lambda t: stepped(pred[h][0], t), lambda t: stepped(ng0, t)])
             e1 = subtract_dealt(f"e{h}1d", pred[h][1], g1)
             bank1 = turn(f"e{h}1", [lambda t: e1[:, t, :]])
-            g_bf = [keep.tile([P, PASS], BF16, name=f"g_bf{h}{a}", align_bytes=64) for a in range(2)]
+            return [bank0, bank1]
+
+        def weigh_errors(h, banks):
+            g_bf = keep.tile([P, 2, PASS], BF16, name=f"g_bf{h}", tag=f"pred{h}1", align_bytes=64)
             for a in range(2):
-                weigh(g_bf[a][:], [bank0, bank1][a], rb_neg[:, a, :])
-            for a in range(2):
-                nc.vector.quantize_mx(out=g_codes[h][a][:].bitcast(E5M2X4), scales=g_scales[h][a][:], in_=g_bf[a][:])
+                weigh(g_bf[:, a, :], banks[a], rb_neg[:, a, :])
+            return g_bf
+
+        banks0 = error_banks(0)
+        u_codes = keep.tile([P, 2, K], U32, name="u_codes", tag="g01", align_bytes=64)
+        nc.vector.quantize_mx(
+            out=u_codes[:].rearrange("p a c -> p (a c)").bitcast(E4M3X4),
+            scales=u_scales[:].rearrange("p a c -> p (a c)"),
+            in_=u_bf[:].rearrange("p a c -> p (a c)"),
+        )
+        g_bf0 = weigh_errors(0, banks0)
+        banks1 = error_banks(1)
+        g_codes = [
+            keep.tile([P, 2, P], U32, name="g_codes0", tag="g11", align_bytes=64),
+            keep.tile([P, 2, P], U32, name="g_codes1", align_bytes=64),
+        ]
+        nc.vector.quantize_mx(
+            out=g_codes[0][:].rearrange("p a c -> p (a c)").bitcast(E5M2X4),
+            scales=g_scales[0][:].rearrange("p a c -> p (a c)"),
+            in_=g_bf0[:].rearrange("p a c -> p (a c)"),
+        )
+        g_bf1 = weigh_errors(1, banks1)
+        for a in range(2):
+            nc.vector.quantize_mx(out=g_codes[1][:, a, :].bitcast(E5M2X4), scales=g_scales[1][:, a, :], in_=g_bf1[:, a, :])
 
         moment = [psum.tile([P, N], F32, name=f"moment{h}", tag=["u00", "u01"][h]) for h in range(2)]
         for nh in range(2):
@@ -157,10 +177,10 @@ def tile_list_moment_gaps_errors_preconditioned_kernel(tc, xf, ra, gt, rb, pr, p
                 for a in range(2):
                     nc.tensor.matmul_mx(
                         out=moment[h][:, nh * P : (nh + 1) * P],
-                        lhsT=u_codes[a][:, h * P : (h + 1) * P].bitcast(E4M3X4),
-                        lhsT_scale=u_scales[a][:, h * P : (h + 1) * P],
-                        rhs=g_codes[nh][a][:].bitcast(E5M2X4),
-                        rhs_scale=g_scales[nh][a][:],
+                        lhsT=u_codes[:, a, h * P : (h + 1) * P].bitcast(E4M3X4),
+                        lhsT_scale=u_scales[:, a, h * P : (h + 1) * P],
+                        rhs=g_codes[nh][:, a, :].bitcast(E5M2X4),
+                        rhs_scale=g_scales[nh][:, a, :],
                         start=(a == 0),
                         stop=(a == 1),
                     )

from contextlib import ExitStack

import concourse.mybir as mybir
from concourse.masks import make_identity

K, J, N, T, V = 256, 1024, 256, 2048, 2048
FLOPS = 2 * K * J * N

F32 = mybir.dt.float32
BF16 = mybir.dt.bfloat16
U32 = mybir.dt.uint32
U16 = mybir.dt.uint16
U8 = mybir.dt.uint8
E4M3X4 = mybir.dt.float8_e4m3fn_x4
E5M2X4 = mybir.dt.float8_e5m2_x4
ALU = mybir.AluOpType
COPY = mybir.ActivationFunctionType.Copy

P = 128
PACK = 4
PASS = P * PACK
LIST_COLS = PASS // 16


def tile_list_moment_gaps_errors_preconditioned_kernel(tc, xf, ra, gt, rb, pr, pc1, old, offs, offs2, offs3, out):
    nc = tc.nc
    with ExitStack() as ctx:
        keep = ctx.enter_context(tc.tile_pool(name="keep", bufs=1))
        psum = ctx.enter_context(tc.psum_pool(name="psum", bufs=1))

        def list_slice(tile, a):
            return tile[:, a * LIST_COLS : (a + 1) * LIST_COLS]

        first = keep.tile([P, J // 16], U16, name="first")
        second = keep.tile([P, J // 16], U16, name="second")
        third = keep.tile([P, J // 16], U16, name="third")
        x_tab = [keep.tile([P, T], F32, name=f"x_tab{h}") for h in range(2)]
        g_tab = [keep.tile([P, V], F32, name=f"g_tab{h}") for h in range(2)]
        pred = [[keep.tile([P, PASS], F32, name=f"pred{h}{a}", align_bytes=64) for a in range(2)] for h in range(2)]
        ra_sb = keep.tile([P, 2, PACK], F32, name="ra_sb")
        rb_sb = keep.tile([P, 2, PACK], F32, name="rb_sb")
        rb_neg = keep.tile([P, 2, PACK], F32, name="rb_neg")
        pc1_sb = keep.tile([P, 2, N], F32, name="pc1_sb")
        old_sb = keep.tile([P, 2, N], F32, name="old_sb")
        ident = keep.tile([P, P], F32, name="ident")

        nc.scalar.dma_start(out=rb_sb[:], in_=rb.rearrange("o (a p t) -> p (o a) t", p=P, t=PACK))
        nc.scalar.dma_start(out=ra_sb[:], in_=ra.rearrange("o (a p t) -> p (o a) t", p=P, t=PACK))
        nc.sync.dma_start(out=x_tab[0][:], in_=xf[0:P, :])
        nc.sync.dma_start(second[:], offs2)
        nc.sync.dma_start(first[:], offs)
        nc.sync.dma_start(out=x_tab[1][:], in_=xf[P : 2 * P, :])
        nc.sync.dma_start(third[:], offs3)
        nc.sync.dma_start(out=g_tab[0][:], in_=gt[0:P, :])
        for a in range(2):
            nc.sync.dma_start(out=pred[0][a][:], in_=pr[0:P, a * PASS : (a + 1) * PASS])
        nc.sync.dma_start(out=g_tab[1][:], in_=gt[P : 2 * P, :])
        for a in range(2):
            nc.sync.dma_start(out=pred[1][a][:], in_=pr[P : 2 * P, a * PASS : (a + 1) * PASS])
        nc.sync.dma_start(out=pc1_sb[:], in_=pc1.rearrange("(h p) n -> p h n", p=P))
        nc.sync.dma_start(out=old_sb[:], in_=old.rearrange("(h p) n -> p h n", p=P))
        make_identity(nc, ident[:])
        nc.scalar.activation(out=rb_neg[:], in_=rb_sb[:], func=COPY, scale=-1.0)

        def gather_scalar(name, table, offsets, scale, tag=""):
            picked = keep.tile([P, PASS], F32, name=name, tag=tag or name, align_bytes=64)
            nc.scalar.activation(out=picked[:], in_=table[:].indirect(offsets), func=COPY, scale=scale)
            return picked

        def gather_vector(name, table, offsets):
            picked = keep.tile([P, PASS], F32, name=name, align_bytes=64)
            nc.vector.tensor_copy(out=picked[:], in_=table[:].indirect(offsets))
            return picked

        def gather_minus(name, table, offsets, other):
            diff = keep.tile([P, PASS], F32, name=name)
            nc.vector.tensor_tensor(out=diff[:], in0=table[:].indirect(offsets), in1=other[:], op=ALU.subtract)
            return diff

        def subtract_dealt(name, left, right):
            diff = keep.tile([P, PACK, P], F32, name=name)
            nc.vector.tensor_tensor(
                out=diff[:].rearrange("p t q -> p q t"),
                in0=left[:].rearrange("p (q t) -> p q t", t=PACK),
                in1=right[:].rearrange("p (q t) -> p q t", t=PACK),
                op=ALU.subtract,
            )
            return diff

        def stepped(tile, t):
            return tile[:, t:PASS:PACK]

        def turn(tag, sources):
            bank = psum.tile([P, PACK, P], F32, name=tag)
            count = len(sources) * PACK
            done = 0
            for source in sources:
                for t in range(PACK):
                    nc.tensor.matmul(
                        out=bank[:, t, :], lhsT=source(t), rhs=ident[:], is_transpose=True,
                        start=(done == 0), stop=(done == count - 1),
                    )
                    done += 1
            return bank

        def weigh(dest, bank, weights):
            nc.vector.tensor_tensor(
                out=dest.rearrange("p (c t) -> p c t", t=PACK),
                in0=bank[:].rearrange("p t c -> p c t"),
                in1=weights.unsqueeze(1).to_broadcast([P, P, PACK]),
                op=ALU.mult,
            )

        u_scales = keep.tile([P, 2, K], U8, name="u_scales", align_bytes=64)
        g_scales = [keep.tile([P, 2, P], U8, name=f"g_scales{h}", align_bytes=64) for h in range(2)]

        b00 = gather_scalar("b00", x_tab[0], list_slice(second, 0), 1.0)
        a01 = gather_vector("a01", x_tab[0], list_slice(first, 1))
        nb01 = gather_scalar("nb01", x_tab[0], list_slice(second, 1), -1.0)
        d00 = gather_minus("d00", x_tab[0], list_slice(first, 0), b00)
        u01 = turn("u01", [lambda t: stepped(a01, t), lambda t: stepped(nb01, t)])
        u00 = turn("u00", [lambda t: stepped(d00, t)])

        b10 = gather_scalar("b10", x_tab[1], list_slice(second, 0), 1.0)
        a11 = gather_vector("a11", x_tab[1], list_slice(first, 1))
        b11 = gather_scalar("b11", x_tab[1], list_slice(second, 1), 1.0)
        d10 = gather_minus("d10", x_tab[1], list_slice(first, 0), b10)
        d11 = subtract_dealt("d11", a11, b11)
        u10 = turn("u10", [lambda t: stepped(d10, t)])
        u11 = turn("u11", [lambda t: d11[:, t, :]])

        u_bf = keep.tile([P, 2, 2 * PASS], BF16, name="u_bf", tag="a11", align_bytes=64)
        weigh(u_bf[:, 1, 0:PASS], u01, ra_sb[:, 1, :])
        weigh(u_bf[:, 0, 0:PASS], u00, ra_sb[:, 0, :])
        weigh(u_bf[:, 0, PASS : 2 * PASS], u10, ra_sb[:, 0, :])
        weigh(u_bf[:, 1, PASS : 2 * PASS], u11, ra_sb[:, 1, :])

        def error_banks(h):
            ng0 = gather_scalar(f"ng{h}0", g_tab[h], list_slice(third, 0), -1.0)
            g1 = gather_scalar(f"g{h}1", g_tab[h], list_slice(third, 1), 1.0)
            bank0 = turn(f"e{h}0", [lambda t: stepped(pred[h][0], t), lambda t: stepped(ng0, t)])
            e1 = subtract_dealt(f"e{h}1d", pred[h][1], g1)
            bank1 = turn(f"e{h}1", [lambda t: e1[:, t, :]])
            return [bank0, bank1]

        def weigh_errors(h, banks):
            g_bf = keep.tile([P, 2, PASS], BF16, name=f"g_bf{h}", tag=f"pred{h}1", align_bytes=64)
            for a in range(2):
                weigh(g_bf[:, a, :], banks[a], rb_neg[:, a, :])
            return g_bf

        banks0 = error_banks(0)
        u_codes = keep.tile([P, 2, K], U32, name="u_codes", tag="g01", align_bytes=64)
        nc.vector.quantize_mx(
            out=u_codes[:].rearrange("p a c -> p (a c)").bitcast(E4M3X4),
            scales=u_scales[:].rearrange("p a c -> p (a c)"),
            in_=u_bf[:].rearrange("p a c -> p (a c)"),
        )
        g_bf0 = weigh_errors(0, banks0)
        banks1 = error_banks(1)
        g_codes = [
            keep.tile([P, 2, P], U32, name="g_codes0", tag="g11", align_bytes=64),
            keep.tile([P, 2, P], U32, name="g_codes1", align_bytes=64),
        ]
        nc.vector.quantize_mx(
            out=g_codes[0][:].rearrange("p a c -> p (a c)").bitcast(E5M2X4),
            scales=g_scales[0][:].rearrange("p a c -> p (a c)"),
            in_=g_bf0[:].rearrange("p a c -> p (a c)"),
        )
        g_bf1 = weigh_errors(1, banks1)
        for a in range(2):
            nc.vector.quantize_mx(out=g_codes[1][:, a, :].bitcast(E5M2X4), scales=g_scales[1][:, a, :], in_=g_bf1[:, a, :])

        moment = [psum.tile([P, N], F32, name=f"moment{h}", tag=["u00", "u01"][h]) for h in range(2)]
        for nh in range(2):
            for h in range(2):
                for a in range(2):
                    nc.tensor.matmul_mx(
                        out=moment[h][:, nh * P : (nh + 1) * P],
                        lhsT=u_codes[:, a, h * P : (h + 1) * P].bitcast(E4M3X4),
                        lhsT_scale=u_scales[:, a, h * P : (h + 1) * P],
                        rhs=g_codes[nh][:, a, :].bitcast(E5M2X4),
                        rhs_scale=g_scales[nh][:, a, :],
                        start=(a == 0),
                        stop=(a == 1),
                    )
        w2_neg = [keep.tile([P, N], F32, name=f"w2_neg{h}") for h in range(2)]
        sums = [keep.tile([P, 1], F32, name=f"sums{h}") for h in range(2)]
        shift = [keep.tile([P, 1], F32, name=f"shift{h}") for h in range(2)]
        res = [keep.tile([P, N], F32, name=f"res{h}") for h in range(2)]
        for h in range(2):
            nc.vector.scalar_tensor_tensor(
                out=w2_neg[h][:], in0=moment[h][:], scalar=-1.0, in1=pc1_sb[:, h, :],
                op0=ALU.mult, op1=ALU.mult, accum_out=sums[h][:],
            )
        for h in range(2):
            nc.vector.tensor_scalar(out=shift[h][:], in0=sums[h][:], scalar1=-0.2 / N, scalar2=None, op0=ALU.mult)
        for h in range(2):
            nc.vector.scalar_tensor_tensor(
                out=res[h][:], in0=w2_neg[h][:], scalar=shift[h][:], in1=old_sb[:, h, :], op0=ALU.add, op1=ALU.add
            )
            [nc.sync, nc.scalar][h].dma_start(out=out[h * P : (h + 1) * P, :], in_=res[h][:])
